import numpy as np
import ml_dtypes


def mxq(x, axis, fmt="e4m3"):
    dtype, down = {"e4m3": (ml_dtypes.float8_e4m3fn, 7), "e5m2": (ml_dtypes.float8_e5m2, 14)}[fmt]
    v = np.moveaxis(np.asarray(x, np.float32).astype(ml_dtypes.bfloat16).astype(np.float64), axis, -1)
    blocks = v.reshape(v.shape[:-1] + (-1, 32))
    amax = np.abs(blocks).max(-1, keepdims=True)
    byte = np.maximum(np.where(amax > 0, np.frexp(amax)[1] - 1 + 127, 0) - down, 1)
    scale = np.exp2(byte - 127.0)
    codes = (blocks / scale).astype(np.float32).astype(dtype).astype(np.float64)
    return np.moveaxis((codes * scale).reshape(v.shape), -1, axis)


WIDE = False


def mx_kscale(k):
    if not WIDE:
        return np.ones(k)
    levels = np.array([10, -10, 5, -5, 0])
    if k % 512:
        return np.exp2(np.random.permutation(np.resize(levels, k // 32))).repeat(32)
    a = np.empty((k // 512, 16))
    for p in range(k // 512):
        a[p, :8] = np.random.permutation(np.resize(levels, 8))
        for g in range(8):
            far = levels[np.abs(levels - a[p, g]) >= 10]
            a[p, g + 8] = far[np.random.randint(len(far))]
    return np.exp2(a.ravel()).repeat(32)


def f64(x):
    return np.asarray(x).astype(np.float64)


def striped(idx):
    return np.tile(idx.reshape(-1, 16).T, (8, 1)).astype(np.uint16)


def unstriped(offs):
    return offs[:16].T.reshape(-1).astype(np.int64)


def relu(v):
    return np.maximum(v, 0.0)


K, T, E, C, N = 512, 1024, 12, 256, 128
TOP = 3


def by_expert(wq, xq):
    return np.concatenate([wq[e].T @ xq[:, e * C:(e + 1) * C] for e in range(E)], axis=1)


def setup_inputs():
    n = np.random.standard_normal
    s = mx_kscale(K)[:, None]
    deal = np.repeat(np.arange(E), C).reshape(TOP, T)[:, np.random.permutation(T)]
    deal = np.take_along_axis(deal, np.argsort(np.random.rand(TOP, T), axis=0), axis=0)
    for _ in range(8):
        s_, t_ = np.random.permutation(T).reshape(2, -1); r = np.random.randint(TOP, size=T // 2); x, y = deal[r, s_].copy(), deal[r, t_].copy()
        ok = ~((deal[:, s_] == y).any(0) | (deal[:, t_] == x).any(0)); deal[r[ok], s_[ok]] = y[ok]; deal[r[ok], t_[ok]] = x[ok]
    order = np.lexsort((np.random.rand(TOP * T), deal.reshape(-1)))
    slot_token = order % T; pos = np.empty(TOP * T, np.int64); pos[order] = np.arange(TOP * T); pos = pos.reshape(TOP, T)
    g = np.random.uniform(0.5, 1.5, (TOP, T)); g = g / g.sum(0)
    w_slot = np.empty(E * C)
    for r in range(TOP): w_slot[pos[r]] = g[r]
    return {
        "xT": (n((K, T)) * s).astype(np.float32),
        "w": (n((E, K, N)) / np.sqrt(K) / s[None]).astype(np.float32),
        "b": (0.3 * n((N, E))).astype(np.float32),
        "gate": np.tile(w_slot, (K, 1)).astype(np.float32),
        "offs": striped(slot_token),
        "pos1": striped(pos[0]),
        "pos2": striped(pos[1]),
        "pos3": striped(pos[2]),
    }


def reference(xT, w, b, gate, offs, pos1, pos2, pos3):
    idx = unstriped(offs)
    xq = mxq(f64(gate) * f64(xT)[:, idx], 0, "e4m3")
    y = by_expert(mxq(f64(w), 1, "e4m3"), xq)
    y = relu(y + np.repeat(f64(b), C, axis=1))
    return y[:, unstriped(pos1)] + y[:, unstriped(pos2)] + y[:, unstriped(pos3)]

@@ -1,0 +1,189 @@
+from contextlib import ExitStack
+
+import concourse.mybir as mybir
+
+K, T, E, C, N = 512, 1024, 12, 256, 128
+S = E * C
+FLOPS = 2 * K * N * S
+
+F32 = mybir.dt.float32
+BF16 = mybir.dt.bfloat16
+U32 = mybir.dt.uint32
+U16 = mybir.dt.uint16
+U8 = mybir.dt.uint8
+FP8X4 = mybir.dt.float8_e4m3fn_x4
+MULT = mybir.AluOpType.mult
+ADD = mybir.AluOpType.add
+RELU = mybir.ActivationFunctionType.Relu
+
+P = 128
+PACK = 4
+PER_COLUMN = 16
+
+HEAD = 1024
+CHUNKS = [(1024, 1536), (1536, 2048), (2048, 2560), (2560, 2816), (2816, 2944), (2944, 3072)]
+W_PAIRS = [(0, 2), (2, 4), (4, 6), (6, 8), (8, 10), (10, 12)]
+TOKEN_PIECES = [(0, 640), (640, 1024)]
+
+
+def tile_moe_pre_lin_relu_kernel(tc, xT, w, b, gate, offs, pos1, pos2, pos3, out):
+    nc = tc.nc
+    x_rows = xT.rearrange("(p j) t -> p j t", j=PACK)
+    gate_rows = gate.rearrange("(p j) s -> p j s", j=PACK)
+    w_rows = w.rearrange("e (p j) n -> p e (j n)", j=PACK)
+
+    with ExitStack() as ctx:
+        lists = ctx.enter_context(tc.tile_pool(name="lists", bufs=1))
+        keep = ctx.enter_context(tc.tile_pool(name="keep", bufs=1))
+        psum = ctx.enter_context(tc.psum_pool(name="psum", bufs=8))
+
+        offs_sb = lists.tile([P, S // PER_COLUMN], U16, name="offs_sb")
+        pos_sb = [lists.tile([P, T // PER_COLUMN], U16, name="pos%d_sb" % r) for r in range(3)]
+        bias = keep.tile([P, E], F32, name="bias")
+        planes = [keep.tile([P, T], F32, name="x_plane%d" % j) for j in range(PACK)]
+        spans = [(0, HEAD)] + CHUNKS
+        gates = {s: keep.tile([P, PACK, s[1] - s[0]], F32, name="gate%d" % s[0]) for s in spans}
+        scaled = {s: keep.tile([P, PACK, s[1] - s[0]], F32, name="scaled%d" % s[0]) for s in spans}
+        x_bf = keep.tile([P, S, PACK], BF16, name="x_bf", align_bytes=64)
+        x_codes = keep.tile([P, S], U32, name="x_codes", align_bytes=64)
+        x_scales = keep.tile([P, S], U8, name="x_scales", align_bytes=64)
+        w_raw = keep.tile([P, E, PACK * N], F32, name="w_raw")
+        w_bf = keep.tile([P, E * N, PACK], BF16, name="w_bf", align_bytes=64)
+        w_codes = keep.tile([P, E * N], U32, name="w_codes", align_bytes=64)
+        w_scales = keep.tile([P, E * N], U8, name="w_scales", align_bytes=64)
+        y = keep.tile([P, S], F32, name="y")
+
+        def load_gate(span, j0, j1, lo, hi):
+            nc.sync.dma_start(gates[span][:, j0:j1, lo - span[0] : hi - span[0]], gate_rows[:, j0:j1, lo:hi])
+
+        def load_w(pair):
+            nc.sync.dma_start(w_raw[:, pair[0] : pair[1], :], w_rows[:, pair[0] : pair[1], :])
+
+        def gather(span, j, lo, hi):
+            cols = slice(lo - span[0], hi - span[0])
+            picked = planes[j][:].indirect(offs_sb[:, lo // PER_COLUMN : hi // PER_COLUMN])
+            nc.vector.tensor_tensor(scaled[span][:, j, cols], picked, gates[span][:, j, cols], MULT)
+
+        def interleave(dst, src):
+            nc.scalar.copy(
+                out=dst.rearrange("p (c i) j -> p c j i", i=4),
+                in_=src.rearrange("p j (c i) -> p c j i", i=4),
+            )
+
+        def round_x(span, lo, hi):
+            interleave(x_bf[:, lo:hi, :], scaled[span][:, :, lo - span[0] : hi - span[0]])
+
+        def round_w(e):
+            interleave(w_bf[:, e * N : (e + 1) * N, :], w_raw[:, e, :].rearrange("p (j n) -> p j n", j=PACK))
+
+        def quantize(codes, scales, src, lo, hi):
+            nc.vector.quantize_mx(
+                out=codes[:, lo:hi].bitcast(FP8X4),
+                scales=scales[:, lo:hi],
+                in_=src[:, lo:hi, :].rearrange("p s j -> p (s j)"),
+            )
+
+        def multiply(lo, hi):
+            for s0 in range(lo, hi, C):
+                s1 = min(s0 + C, hi)
+                e = s0 // C
+                acc = psum.tile([P, s1 - s0], F32, name="acc")
+                nc.tensor.matmul_mx(
+                    out=acc[:],
+                    lhsT=w_codes[:, e * N : (e + 1) * N].bitcast(FP8X4),
+                    lhsT_scale=w_scales[:, e * N : (e + 1) * N],
+                    rhs=x_codes[:, s0:s1].bitcast(FP8X4),
+                    rhs_scale=x_scales[:, s0:s1],
+                    start=True,
+                    stop=True,
+                )
+                nc.scalar.activation(y[:, s0:s1], acc[:], RELU, bias=bias[:, e : e + 1])
+
+        head = spans[0]
+
+        nc.sync.dma_start(planes[0][:], x_rows[:, 0, :])
+        nc.sync.dma_start(offs_sb[:], offs)
+        load_gate(head, 0, 1, 0, 256)
+        load_gate(head, 0, 1, 256, 512)
+        load_gate(head, 0, 1, 512, 1024)
+        for j in range(1, PACK):
+            nc.sync.dma_start(planes[j][:], x_rows[:, j, :])
+            load_gate(head, j, j + 1, 0, 512)
+            load_gate(head, j, j + 1, 512, 1024)
+        load_gate(CHUNKS[0], 0, 2, CHUNKS[0][0], CHUNKS[0][1])
+        load_w(W_PAIRS[0])
+        load_gate(CHUNKS[0], 2, 4, CHUNKS[0][0], CHUNKS[0][1])
+        load_w(W_PAIRS[1])
+        nc.sync.dma_start(bias[:], b)
+        for i in range(1, len(CHUNKS)):
+            load_gate(CHUNKS[i], 0, PACK, CHUNKS[i][0], CHUNKS[i][1])
+            if i + 1 < len(W_PAIRS):
+                load_w(W_PAIRS[i + 1])
+        for r, pos in enumerate((pos1, pos2, pos3)):
+            nc.sync.dma_start(pos_sb[r][:], pos)
+
+        gather(head, 0, 0, 256)
+        gather(head, 0, 256, 512)
+        gather(head, 0, 512, 1024)
+        for j in (1, 2):
+            gather(head, j, 0, 512)
+            gather(head, j, 512, 1024)
+        for lo, hi in ((0, 256), (256, 512), (512, 1024)):
+            gather(head, 3, lo, hi)
+            round_x(head, lo, hi)
+        for e in range(0, 4):
+            round_w(e)
+
+        def finish(span):
+            for lo in range(span[0], span[1], 512):
+                hi = min(lo + 512, span[1])
+                quantize(x_codes, x_scales, x_bf, lo, hi)
+                multiply(lo, hi)
+
+        def start(span):
+            for j in range(PACK):
+                gather(span, j, span[0], span[1])
+            round_x(span, span[0], span[1])
+
+        start(CHUNKS[0])
+        quantize(w_codes, w_scales, w_bf, 0, 4 * N)
+        finish(head)
+        for i in range(1, 4):
+            round_w(2 * i + 2)
+            round_w(2 * i + 3)
+            start(CHUNKS[i])
+            quantize(w_codes, w_scales, w_bf, (2 * i + 2) * N, (2 * i + 4) * N)
+            finish(CHUNKS[i - 1])
+        round_w(10)
+        round_w(11)
+        start(CHUNKS[4])
+        start(CHUNKS[5])
+        quantize(w_codes, w_scales, w_bf, 10 * N, 12 * N)
+        for span in CHUNKS[3:]:
+            finish(span)
+
+        (a0, a1), (b0, b1) = TOKEN_PIECES
+        fetched = {}
+        for lo, hi in TOKEN_PIECES:
+            for r in range(3):
+                fetched[lo, r] = keep.tile([P, hi - lo], F32, name="fetched%d_%d" % (lo, r))
+
+        def fetch(lo, hi, r):
+            picked = y[:].indirect(pos_sb[r][:, lo // PER_COLUMN : hi // PER_COLUMN])
+            nc.vector.tensor_copy(fetched[lo, r][:], picked)
+
+        def add(lo, r):
+            nc.vector.tensor_tensor(fetched[lo, 0][:], fetched[lo, 0][:], fetched[lo, r][:], ADD)
+
+        fetch(a0, a1, 0)
+        fetch(a0, a1, 1)
+        fetch(a0, a1, 2)
+        add(a0, 1)
+        fetch(b0, b1, 0)
+        add(a0, 2)
+        nc.sync.dma_start(out[:, a0:a1], fetched[a0, 0][:])
+        fetch(b0, b1, 1)
+        fetch(b0, b1, 2)
+        add(b0, 1)
+        add(b0, 2)
+        nc.sync.dma_start(out[:, b0:b1], fetched[b0, 0][:])

@@ -20,16 +20,14 @@ P = 128
 PACK = 4
 PER_COLUMN = 16
 
-HEAD = 1024
-CHUNKS = [(1024, 1536), (1536, 2048), (2048, 2560), (2560, 2816), (2816, 2944), (2944, 3072)]
-W_PAIRS = [(0, 2), (2, 4), (4, 6), (6, 8), (8, 10), (10, 12)]
+CHUNKS = [(0, 512), (512, 1024), (1024, 1536), (1536, 2048), (2048, 2560), (2560, 2816), (2816, 2944), (2944, 3072)]
 TOKEN_PIECES = [(0, 640), (640, 1024)]
+TAKES_OVER = {2: 0, 3: 1, 4: 2, 5: 3, 7: 4}
 
 
 def tile_moe_pre_lin_relu_kernel(tc, xT, w, b, gate, offs, pos1, pos2, pos3, out):
     nc = tc.nc
     x_rows = xT.rearrange("(p j) t -> p j t", j=PACK)
-    gate_rows = gate.rearrange("(p j) s -> p j s", j=PACK)
     w_rows = w.rearrange("e (p j) n -> p e (j n)", j=PACK)
 
     with ExitStack() as ctx:
@@ -41,10 +39,7 @@ def tile_moe_pre_lin_relu_kernel(tc, xT, w, b, gate, offs, pos1, pos2, pos3, out
         pos_sb = [lists.tile([P, T // PER_COLUMN], U16, name="pos%d_sb" % r) for r in range(3)]
         bias = keep.tile([P, E], F32, name="bias")
         planes = [keep.tile([P, T], F32, name="x_plane%d" % j) for j in range(PACK)]
-        spans = [(0, HEAD)] + CHUNKS
-        gates = {s: keep.tile([P, PACK, s[1] - s[0]], F32, name="gate%d" % s[0]) for s in spans}
-        scaled = {s: keep.tile([P, PACK, s[1] - s[0]], F32, name="scaled%d" % s[0]) for s in spans}
-        x_bf = keep.tile([P, S, PACK], BF16, name="x_bf", align_bytes=64)
+        gates = keep.tile([P, S], F32, name="gates")
         x_codes = keep.tile([P, S], U32, name="x_codes", align_bytes=64)
         x_scales = keep.tile([P, S], U8, name="x_scales", align_bytes=64)
         w_raw = keep.tile([P, E, PACK * N], F32, name="w_raw")
@@ -52,17 +47,13 @@ def tile_moe_pre_lin_relu_kernel(tc, xT, w, b, gate, offs, pos1, pos2, pos3, out
         w_codes = keep.tile([P, E * N], U32, name="w_codes", align_bytes=64)
         w_scales = keep.tile([P, E * N], U8, name="w_scales", align_bytes=64)
         y = keep.tile([P, S], F32, name="y")
+        x_bf = {}
 
-        def load_gate(span, j0, j1, lo, hi):
-            nc.sync.dma_start(gates[span][:, j0:j1, lo - span[0] : hi - span[0]], gate_rows[:, j0:j1, lo:hi])
+        def load_gate(lo, hi):
+            nc.sync.dma_start(gates[:, lo:hi], gate[0:P, lo:hi])
 
-        def load_w(pair):
-            nc.sync.dma_start(w_raw[:, pair[0] : pair[1], :], w_rows[:, pair[0] : pair[1], :])
-
-        def gather(span, j, lo, hi):
-            cols = slice(lo - span[0], hi - span[0])
-            picked = planes[j][:].indirect(offs_sb[:, lo // PER_COLUMN : hi // PER_COLUMN])
-            nc.vector.tensor_tensor(scaled[span][:, j, cols], picked, gates[span][:, j, cols], MULT)
+        def load_w(e0, e1):
+            nc.sync.dma_start(w_raw[:, e0:e1, :], w_rows[:, e0:e1, :])
 
         def interleave(dst, src):
             nc.scalar.copy(
@@ -70,20 +61,36 @@ def tile_moe_pre_lin_relu_kernel(tc, xT, w, b, gate, offs, pos1, pos2, pos3, out
                 in_=src.rearrange("p j (c i) -> p c j i", i=4),
             )
 
-        def round_x(span, lo, hi):
-            interleave(x_bf[:, lo:hi, :], scaled[span][:, :, lo - span[0] : hi - span[0]])
+        def gather(c):
+            lo, hi = CHUNKS[c]
+            tag = "rounded%d" % TAKES_OVER[c] if c in TAKES_OVER else "scaled%d" % c
+            scaled = keep.tile([P, PACK, hi - lo], F32, name="scaled%d" % c, tag=tag, align_bytes=64)
+            for j in range(PACK):
+                step = 256 if (c, j) == (0, 0) else hi - lo
+                for s0 in range(lo, hi, step):
+                    s1 = s0 + step
+                    picked = planes[j][:].indirect(offs_sb[:, s0 // PER_COLUMN : s1 // PER_COLUMN])
+                    nc.vector.tensor_tensor(scaled[:, j, s0 - lo : s1 - lo], picked, gates[:, s0:s1], MULT)
+            x_bf[c] = keep.tile([P, hi - lo, PACK], BF16, name="rounded%d" % c, tag="rounded%d" % c, align_bytes=64)
+            interleave(x_bf[c][:], scaled[:])
 
-        def round_w(e):
-            interleave(w_bf[:, e * N : (e + 1) * N, :], w_raw[:, e, :].rearrange("p (j n) -> p j n", j=PACK))
+        def round_w(e0, e1):
+            for e in range(e0, e1):
+                interleave(w_bf[:, e * N : (e + 1) * N, :], w_raw[:, e, :].rearrange("p (j n) -> p j n", j=PACK))
 
-        def quantize(codes, scales, src, lo, hi):
-            nc.vector.quantize_mx(
-                out=codes[:, lo:hi].bitcast(FP8X4),
-                scales=scales[:, lo:hi],
-                in_=src[:, lo:hi, :].rearrange("p s j -> p (s j)"),
-            )
+        def quantize(codes, scales, src):
+            nc.vector.quantize_mx(out=codes.bitcast(FP8X4), scales=scales, in_=src.rearrange("p s j -> p (s j)"))
 
-        def multiply(lo, hi):
+        def quantize_w(e0, e1):
+            cols = slice(e0 * N, e1 * N)
+            quantize(w_codes[:, cols], w_scales[:, cols], w_bf[:, cols, :])
+
+        def quantize_x(c):
+            lo, hi = CHUNKS[c]
+            quantize(x_codes[:, lo:hi], x_scales[:, lo:hi], x_bf[c][:])
+
+        def multiply(c):
+            lo, hi = CHUNKS[c]
             for s0 in range(lo, hi, C):
                 s1 = min(s0 + C, hi)
                 e = s0 // C
@@ -99,68 +106,43 @@ def tile_moe_pre_lin_relu_kernel(tc, xT, w, b, gate, offs, pos1, pos2, pos3, out
                 )
                 nc.scalar.activation(y[:, s0:s1], acc[:], RELU, bias=bias[:, e : e + 1])
 
-        head = spans[0]
-
         nc.sync.dma_start(planes[0][:], x_rows[:, 0, :])
         nc.sync.dma_start(offs_sb[:], offs)
-        load_gate(head, 0, 1, 0, 256)
-        load_gate(head, 0, 1, 256, 512)
-        load_gate(head, 0, 1, 512, 1024)
+        load_gate(0, 256)
+        load_gate(256, 512)
         for j in range(1, PACK):
             nc.sync.dma_start(planes[j][:], x_rows[:, j, :])
-            load_gate(head, j, j + 1, 0, 512)
-            load_gate(head, j, j + 1, 512, 1024)
-        load_gate(CHUNKS[0], 0, 2, CHUNKS[0][0], CHUNKS[0][1])
-        load_w(W_PAIRS[0])
-        load_gate(CHUNKS[0], 2, 4, CHUNKS[0][0], CHUNKS[0][1])
-        load_w(W_PAIRS[1])
+        load_gate(512, 1024)
+        load_w(0, 2)
+        load_w(2, 4)
+        load_gate(1024, 2048)
         nc.sync.dma_start(bias[:], b)
-        for i in range(1, len(CHUNKS)):
-            load_gate(CHUNKS[i], 0, PACK, CHUNKS[i][0], CHUNKS[i][1])
-            if i + 1 < len(W_PAIRS):
-                load_w(W_PAIRS[i + 1])
+        load_w(4, 8)
+        load_gate(2048, 3072)
+        load_w(8, 12)
         for r, pos in enumerate((pos1, pos2, pos3)):
             nc.sync.dma_start(pos_sb[r][:], pos)
 
-        gather(head, 0, 0, 256)
-        gather(head, 0, 256, 512)
-        gather(head, 0, 512, 1024)
-        for j in (1, 2):
-            gather(head, j, 0, 512)
-            gather(head, j, 512, 1024)
-        for lo, hi in ((0, 256), (256, 512), (512, 1024)):
-            gather(head, 3, lo, hi)
-            round_x(head, lo, hi)
-        for e in range(0, 4):
-            round_w(e)
-
-        def finish(span):
-            for lo in range(span[0], span[1], 512):
-                hi = min(lo + 512, span[1])
-                quantize(x_codes, x_scales, x_bf, lo, hi)
-                multiply(lo, hi)
-
-        def start(span):
-            for j in range(PACK):
-                gather(span, j, span[0], span[1])
-            round_x(span, span[0], span[1])
-
-        start(CHUNKS[0])
-        quantize(w_codes, w_scales, w_bf, 0, 4 * N)
-        finish(head)
-        for i in range(1, 4):
-            round_w(2 * i + 2)
-            round_w(2 * i + 3)
-            start(CHUNKS[i])
-            quantize(w_codes, w_scales, w_bf, (2 * i + 2) * N, (2 * i + 4) * N)
-            finish(CHUNKS[i - 1])
-        round_w(10)
-        round_w(11)
-        start(CHUNKS[4])
-        start(CHUNKS[5])
-        quantize(w_codes, w_scales, w_bf, 10 * N, 12 * N)
-        for span in CHUNKS[3:]:
-            finish(span)
+        gather(0)
+        round_w(0, 4)
+        w_steps = {1: (4, 7), 2: (7, 10), 3: (10, 12)}
+        for c in range(1, 5):
+            gather(c)
+            quantize_x(c - 1)
+            quantize_w(2 * c - 2, 2 * c)
+            multiply(c - 1)
+            if c in w_steps:
+                round_w(w_steps[c][0], w_steps[c][1])
+        gather(5)
+        quantize_w(8, 10)
+        gather(6)
+        quantize_x(4)
+        quantize_w(10, 12)
+        multiply(4)
+        gather(7)
+        for c in (5, 6, 7):
+            quantize_x(c)
+            multiply(c)
 
         (a0, a1), (b0, b1) = TOKEN_PIECES
         fetched = {}
@@ -172,18 +154,20 @@ def tile_moe_pre_lin_relu_kernel(tc, xT, w, b, gate, offs, pos1, pos2, pos3, out
             picked = y[:].indirect(pos_sb[r][:, lo // PER_COLUMN : hi // PER_COLUMN])
             nc.vector.tensor_copy(fetched[lo, r][:], picked)
 
-        def add(lo, r):
-            nc.vector.tensor_tensor(fetched[lo, 0][:], fetched[lo, 0][:], fetched[lo, r][:], ADD)
+        def add(engine, piece, r, lo, hi):
+            total = fetched[piece, 0][:, lo:hi]
+            engine.tensor_tensor(total, total, fetched[piece, r][:, lo:hi], ADD)
 
         fetch(a0, a1, 0)
         fetch(a0, a1, 1)
         fetch(a0, a1, 2)
-        add(a0, 1)
         fetch(b0, b1, 0)
-        add(a0, 2)
-        nc.sync.dma_start(out[:, a0:a1], fetched[a0, 0][:])
+        add(nc.vector, a0, 1, 0, a1 - a0)
         fetch(b0, b1, 1)
+        add(nc.vector, a0, 2, 0, a1 - a0)
+        nc.sync.dma_start(out[:, a0:a1], fetched[a0, 0][:])
+        add(nc.vector, b0, 1, 0, b1 - b0)
         fetch(b0, b1, 2)
-        add(b0, 1)
-        add(b0, 2)
-        nc.sync.dma_start(out[:, b0:b1], fetched[b0, 0][:])
+        for lo, hi in ((0, 256), (256, 384)):
+            add(nc.vector, b0, 2, lo, hi)
+            nc.sync.dma_start(out[:, b0 + lo : b0 + hi], fetched[b0, 0][:, lo:hi])

@@ -160,13 +160,13 @@ def tile_moe_pre_lin_relu_kernel(tc, xT, w, b, gate, offs, pos1, pos2, pos3, out
 
         fetch(a0, a1, 0)
         fetch(a0, a1, 1)
+        add(nc.gpsimd, a0, 1, 0, a1 - a0)
         fetch(a0, a1, 2)
-        fetch(b0, b1, 0)
-        add(nc.vector, a0, 1, 0, a1 - a0)
-        fetch(b0, b1, 1)
-        add(nc.vector, a0, 2, 0, a1 - a0)
+        add(nc.gpsimd, a0, 2, 0, a1 - a0)
         nc.sync.dma_start(out[:, a0:a1], fetched[a0, 0][:])
-        add(nc.vector, b0, 1, 0, b1 - b0)
+        fetch(b0, b1, 0)
+        fetch(b0, b1, 1)
+        add(nc.gpsimd, b0, 1, 0, b1 - b0)
         fetch(b0, b1, 2)
         for lo, hi in ((0, 256), (256, 384)):
             add(nc.vector, b0, 2, lo, hi)

@@ -4,6 +4,7 @@ import concourse.mybir as mybir
 
 K, T, E, C, N = 512, 1024, 12, 256, 128
 S = E * C
+TOP = 3
 FLOPS = 2 * K * N * S
 
 F32 = mybir.dt.float32
@@ -18,11 +19,21 @@ RELU = mybir.ActivationFunctionType.Relu
 
 P = 128
 PACK = 4
-PER_COLUMN = 16
+ENTRIES = 16
+RUN = 4
+PAIR = 2
 
-CHUNKS = [(0, 512), (512, 1024), (1024, 1536), (1536, 2048), (2048, 2560), (2560, 2816), (2816, 2944), (2944, 3072)]
-TOKEN_PIECES = [(0, 640), (640, 1024)]
-TAKES_OVER = {2: 0, 3: 1, 4: 2, 5: 3, 7: 4}
+WIDE = PAIR * C
+WIDE_CHUNKS = E // PAIR - 1
+WIDTHS = [WIDE] * WIDE_CHUNKS + [C, C // 2, C // 2]
+CHUNKS = [(sum(WIDTHS[:c]), sum(WIDTHS[: c + 1])) for c in range(len(WIDTHS))]
+LAST = len(CHUNKS) - 1
+
+REUSES = {c: c - 2 for c in range(2, WIDE_CHUNKS + 1)} | {LAST: WIDE_CHUNKS - 1}
+
+W_ROUNDS = [(0, 4), (4, 7), (7, 10), (10, 12)]
+
+SPLIT = 640
 
 
 def tile_moe_pre_lin_relu_kernel(tc, xT, w, b, gate, offs, pos1, pos2, pos3, out):
@@ -35,19 +46,19 @@ def tile_moe_pre_lin_relu_kernel(tc, xT, w, b, gate, offs, pos1, pos2, pos3, out
         keep = ctx.enter_context(tc.tile_pool(name="keep", bufs=1))
         psum = ctx.enter_context(tc.psum_pool(name="psum", bufs=8))
 
-        offs_sb = lists.tile([P, S // PER_COLUMN], U16, name="offs_sb")
-        pos_sb = [lists.tile([P, T // PER_COLUMN], U16, name="pos%d_sb" % r) for r in range(3)]
+        offs_sb = lists.tile([P, S // ENTRIES], U16, name="offs_sb")
+        pos_sb = [lists.tile([P, T // ENTRIES], U16, name="pos%d_sb" % r) for r in range(TOP)]
         bias = keep.tile([P, E], F32, name="bias")
-        planes = [keep.tile([P, T], F32, name="x_plane%d" % j) for j in range(PACK)]
+        tokens = [keep.tile([P, T], F32, name="tokens%d" % j, tag="tokens%d" % j, align_bytes=64) for j in range(PACK)]
         gates = keep.tile([P, S], F32, name="gates")
         x_codes = keep.tile([P, S], U32, name="x_codes", align_bytes=64)
         x_scales = keep.tile([P, S], U8, name="x_scales", align_bytes=64)
         w_raw = keep.tile([P, E, PACK * N], F32, name="w_raw")
-        w_bf = keep.tile([P, E * N, PACK], BF16, name="w_bf", align_bytes=64)
-        w_codes = keep.tile([P, E * N], U32, name="w_codes", align_bytes=64)
+        w_rounded = keep.tile([P, E * N, PACK], BF16, name="w_rounded", align_bytes=64)
         w_scales = keep.tile([P, E * N], U8, name="w_scales", align_bytes=64)
         y = keep.tile([P, S], F32, name="y")
-        x_bf = {}
+        x_rounded = {}
+        w_codes = {}
 
         def load_gate(lo, hi):
             nc.sync.dma_start(gates[:, lo:hi], gate[0:P, lo:hi])
@@ -55,49 +66,53 @@ def tile_moe_pre_lin_relu_kernel(tc, xT, w, b, gate, offs, pos1, pos2, pos3, out
         def load_w(e0, e1):
             nc.sync.dma_start(w_raw[:, e0:e1, :], w_rows[:, e0:e1, :])
 
-        def interleave(dst, src):
+        def round_and_interleave(dst, src):
             nc.scalar.copy(
-                out=dst.rearrange("p (c i) j -> p c j i", i=4),
-                in_=src.rearrange("p j (c i) -> p c j i", i=4),
+                out=dst.rearrange("p (c i) j -> p c j i", i=RUN),
+                in_=src.rearrange("p j (c i) -> p c j i", i=RUN),
             )
 
         def gather(c):
             lo, hi = CHUNKS[c]
-            tag = "rounded%d" % TAKES_OVER[c] if c in TAKES_OVER else "scaled%d" % c
-            scaled = keep.tile([P, PACK, hi - lo], F32, name="scaled%d" % c, tag=tag, align_bytes=64)
+            tag = "rounded%d" % REUSES[c] if c in REUSES else "gathered%d" % c
+            gathered = keep.tile([P, PACK, hi - lo], F32, name="gathered%d" % c, tag=tag, align_bytes=64)
             for j in range(PACK):
-                step = 256 if (c, j) == (0, 0) else hi - lo
+                step = (hi - lo) // 2 if (c, j) == (0, 0) else hi - lo
                 for s0 in range(lo, hi, step):
                     s1 = s0 + step
-                    picked = planes[j][:].indirect(offs_sb[:, s0 // PER_COLUMN : s1 // PER_COLUMN])
-                    nc.vector.tensor_tensor(scaled[:, j, s0 - lo : s1 - lo], picked, gates[:, s0:s1], MULT)
-            x_bf[c] = keep.tile([P, hi - lo, PACK], BF16, name="rounded%d" % c, tag="rounded%d" % c, align_bytes=64)
-            interleave(x_bf[c][:], scaled[:])
+                    picked = tokens[j][:].indirect(offs_sb[:, s0 // ENTRIES : s1 // ENTRIES])
+                    nc.vector.tensor_tensor(gathered[:, j, s0 - lo : s1 - lo], picked, gates[:, s0:s1], MULT)
+            x_rounded[c] = keep.tile([P, hi - lo, PACK], BF16, name="rounded%d" % c, tag="rounded%d" % c, align_bytes=64)
+            round_and_interleave(x_rounded[c][:], gathered[:])
 
         def round_w(e0, e1):
             for e in range(e0, e1):
-                interleave(w_bf[:, e * N : (e + 1) * N, :], w_raw[:, e, :].rearrange("p (j n) -> p j n", j=PACK))
+                src = w_raw[:, e, :].rearrange("p (j n) -> p j n", j=PACK)
+                round_and_interleave(w_rounded[:, e * N : (e + 1) * N, :], src)
 
-        def quantize(codes, scales, src):
-            nc.vector.quantize_mx(out=codes.bitcast(FP8X4), scales=scales, in_=src.rearrange("p s j -> p (s j)"))
+        def quantize(codes, scales, rounded):
+            nc.vector.quantize_mx(out=codes.bitcast(FP8X4), scales=scales, in_=rounded.rearrange("p c j -> p (c j)"))
 
-        def quantize_w(e0, e1):
-            cols = slice(e0 * N, e1 * N)
-            quantize(w_codes[:, cols], w_scales[:, cols], w_bf[:, cols, :])
+        def quantize_w(pair):
+            cols = slice(pair * PAIR * N, (pair + 1) * PAIR * N)
+            tag = "tokens2" if pair == WIDE_CHUNKS else "w_codes%d" % pair
+            w_codes[pair] = keep.tile([P, PAIR * N], U32, name="w_codes%d" % pair, tag=tag, align_bytes=64)
+            quantize(w_codes[pair][:], w_scales[:, cols], w_rounded[:, cols, :])
 
         def quantize_x(c):
             lo, hi = CHUNKS[c]
-            quantize(x_codes[:, lo:hi], x_scales[:, lo:hi], x_bf[c][:])
+            quantize(x_codes[:, lo:hi], x_scales[:, lo:hi], x_rounded[c][:])
 
         def multiply(c):
             lo, hi = CHUNKS[c]
             for s0 in range(lo, hi, C):
                 s1 = min(s0 + C, hi)
                 e = s0 // C
+                pair, place = divmod(e, PAIR)
                 acc = psum.tile([P, s1 - s0], F32, name="acc")
                 nc.tensor.matmul_mx(
                     out=acc[:],
-                    lhsT=w_codes[:, e * N : (e + 1) * N].bitcast(FP8X4),
+                    lhsT=w_codes[pair][:, place * N : (place + 1) * N].bitcast(FP8X4),
                     lhsT_scale=w_scales[:, e * N : (e + 1) * N],
                     rhs=x_codes[:, s0:s1].bitcast(FP8X4),
                     rhs_scale=x_scales[:, s0:s1],
@@ -106,68 +121,72 @@ def tile_moe_pre_lin_relu_kernel(tc, xT, w, b, gate, offs, pos1, pos2, pos3, out
                 )
                 nc.scalar.activation(y[:, s0:s1], acc[:], RELU, bias=bias[:, e : e + 1])
 
-        nc.sync.dma_start(planes[0][:], x_rows[:, 0, :])
+        nc.sync.dma_start(tokens[0][:], x_rows[:, 0, :])
         nc.sync.dma_start(offs_sb[:], offs)
-        load_gate(0, 256)
-        load_gate(256, 512)
+        load_gate(0, WIDE // 2)
+        load_gate(WIDE // 2, WIDE)
         for j in range(1, PACK):
-            nc.sync.dma_start(planes[j][:], x_rows[:, j, :])
-        load_gate(512, 1024)
-        load_w(0, 2)
-        load_w(2, 4)
-        load_gate(1024, 2048)
+            nc.sync.dma_start(tokens[j][:], x_rows[:, j, :])
+        load_gate(WIDE, 2 * WIDE)
+        load_w(0, PAIR)
+        load_w(PAIR, 2 * PAIR)
+        load_gate(2 * WIDE, 4 * WIDE)
         nc.sync.dma_start(bias[:], b)
-        load_w(4, 8)
-        load_gate(2048, 3072)
-        load_w(8, 12)
+        load_w(2 * PAIR, 4 * PAIR)
+        load_gate(4 * WIDE, S)
+        load_w(4 * PAIR, E)
         for r, pos in enumerate((pos1, pos2, pos3)):
             nc.sync.dma_start(pos_sb[r][:], pos)
 
         gather(0)
-        round_w(0, 4)
-        w_steps = {1: (4, 7), 2: (7, 10), 3: (10, 12)}
-        for c in range(1, 5):
+        round_w(*W_ROUNDS[0])
+        for c in range(1, WIDE_CHUNKS):
             gather(c)
             quantize_x(c - 1)
-            quantize_w(2 * c - 2, 2 * c)
+            quantize_w(c - 1)
             multiply(c - 1)
-            if c in w_steps:
-                round_w(w_steps[c][0], w_steps[c][1])
-        gather(5)
-        quantize_w(8, 10)
-        gather(6)
-        quantize_x(4)
-        quantize_w(10, 12)
-        multiply(4)
-        gather(7)
-        for c in (5, 6, 7):
+            if c < len(W_ROUNDS):
+                round_w(*W_ROUNDS[c])
+
+        last_wide = WIDE_CHUNKS - 1
+        gather(last_wide + 1)
+        quantize_w(last_wide)
+        gather(last_wide + 2)
+        quantize_x(last_wide)
+        multiply(last_wide)
+        gather(LAST)
+        quantize_x(last_wide + 1)
+        quantize_w(last_wide + 1)
+        multiply(last_wide + 1)
+        for c in range(last_wide + 2, LAST + 1):
             quantize_x(c)
             multiply(c)
 
-        (a0, a1), (b0, b1) = TOKEN_PIECES
-        fetched = {}
-        for lo, hi in TOKEN_PIECES:
-            for r in range(3):
-                fetched[lo, r] = keep.tile([P, hi - lo], F32, name="fetched%d_%d" % (lo, r))
+        pieces = ((0, SPLIT), (SPLIT, T))
+        results = [
+            [keep.tile([P, hi - lo], F32, name="results%d_%d" % (lo, r)) for r in range(TOP)] for lo, hi in pieces
+        ]
 
-        def fetch(lo, hi, r):
-            picked = y[:].indirect(pos_sb[r][:, lo // PER_COLUMN : hi // PER_COLUMN])
-            nc.vector.tensor_copy(fetched[lo, r][:], picked)
+        def fetch(piece, r):
+            lo, hi = pieces[piece]
+            picked = y[:].indirect(pos_sb[r][:, lo // ENTRIES : hi // ENTRIES])
+            nc.vector.tensor_copy(results[piece][r][:], picked)
 
-        def add(engine, piece, r, lo, hi):
-            total = fetched[piece, 0][:, lo:hi]
-            engine.tensor_tensor(total, total, fetched[piece, r][:, lo:hi], ADD)
+        def add(engine, piece, r, cols):
+            total = results[piece][0][:, cols]
+            engine.tensor_tensor(total, total, results[piece][r][:, cols], ADD)
 
-        fetch(a0, a1, 0)
-        fetch(a0, a1, 1)
-        add(nc.gpsimd, a0, 1, 0, a1 - a0)
-        fetch(a0, a1, 2)
-        add(nc.gpsimd, a0, 2, 0, a1 - a0)
-        nc.sync.dma_start(out[:, a0:a1], fetched[a0, 0][:])
-        fetch(b0, b1, 0)
-        fetch(b0, b1, 1)
-        add(nc.gpsimd, b0, 1, 0, b1 - b0)
-        fetch(b0, b1, 2)
-        for lo, hi in ((0, 256), (256, 384)):
-            add(nc.vector, b0, 2, lo, hi)
-            nc.sync.dma_start(out[:, b0 + lo : b0 + hi], fetched[b0, 0][:, lo:hi])
+        fetch(0, 0)
+        for r in range(1, TOP):
+            fetch(0, r)
+            add(nc.gpsimd, 0, r, slice(0, SPLIT))
+        nc.sync.dma_start(out[:, 0:SPLIT], results[0][0][:])
+
+        for r in range(TOP):
+            fetch(1, r)
+        half = (T - SPLIT) // 2
+        for r in range(1, TOP):
+            for lo in (0, half):
+                add(nc.vector, 1, r, slice(lo, lo + half))
+                if r == TOP - 1:
+                    nc.sync.dma_start(out[:, SPLIT + lo : SPLIT + lo + half], results[1][0][:, lo : lo + half])

from contextlib import ExitStack

import concourse.mybir as mybir

K, T, E, C, N = 512, 1024, 12, 256, 128
S = E * C
TOP = 3
FLOPS = 2 * K * N * S

F32 = mybir.dt.float32
BF16 = mybir.dt.bfloat16
U32 = mybir.dt.uint32
U16 = mybir.dt.uint16
U8 = mybir.dt.uint8
FP8X4 = mybir.dt.float8_e4m3fn_x4
MULT = mybir.AluOpType.mult
ADD = mybir.AluOpType.add
RELU = mybir.ActivationFunctionType.Relu

P = 128
PACK = 4
ENTRIES = 16
RUN = 4
PAIR = 2

WIDE = PAIR * C
WIDE_CHUNKS = E // PAIR - 1
WIDTHS = [WIDE] * WIDE_CHUNKS + [C, C // 2, C // 2]
CHUNKS = [(sum(WIDTHS[:c]), sum(WIDTHS[: c + 1])) for c in range(len(WIDTHS))]
LAST = len(CHUNKS) - 1

REUSES = {c: c - 2 for c in range(2, WIDE_CHUNKS + 1)} | {LAST: WIDE_CHUNKS - 1}

W_ROUNDS = [(0, 4), (4, 7), (7, 10), (10, 12)]

SPLIT = 640


def tile_moe_pre_lin_relu_kernel(tc, xT, w, b, gate, offs, pos1, pos2, pos3, out):
    nc = tc.nc
    x_rows = xT.rearrange("(p j) t -> p j t", j=PACK)
    w_rows = w.rearrange("e (p j) n -> p e (j n)", j=PACK)

    with ExitStack() as ctx:
        lists = ctx.enter_context(tc.tile_pool(name="lists", bufs=1))
        keep = ctx.enter_context(tc.tile_pool(name="keep", bufs=1))
        psum = ctx.enter_context(tc.psum_pool(name="psum", bufs=8))

        offs_sb = lists.tile([P, S // ENTRIES], U16, name="offs_sb")
        pos_sb = [lists.tile([P, T // ENTRIES], U16, name="pos%d_sb" % r) for r in range(TOP)]
        bias = keep.tile([P, E], F32, name="bias")
        tokens = [keep.tile([P, T], F32, name="tokens%d" % j, tag="tokens%d" % j, align_bytes=64) for j in range(PACK)]
        gates = keep.tile([P, S], F32, name="gates")
        x_codes = keep.tile([P, S], U32, name="x_codes", align_bytes=64)
        x_scales = keep.tile([P, S], U8, name="x_scales", align_bytes=64)
        w_raw = keep.tile([P, E, PACK * N], F32, name="w_raw")
        w_rounded = keep.tile([P, E * N, PACK], BF16, name="w_rounded", align_bytes=64)
        w_scales = keep.tile([P, E * N], U8, name="w_scales", align_bytes=64)
        y = keep.tile([P, S], F32, name="y")
        x_rounded = {}
        w_codes = {}

        def load_gate(lo, hi):
            nc.sync.dma_start(gates[:, lo:hi], gate[0:P, lo:hi])

        def load_w(e0, e1):
            nc.sync.dma_start(w_raw[:, e0:e1, :], w_rows[:, e0:e1, :])

        def round_and_interleave(dst, src):
            nc.scalar.copy(
                out=dst.rearrange("p (c i) j -> p c j i", i=RUN),
                in_=src.rearrange("p j (c i) -> p c j i", i=RUN),
            )

        def gather(c):
            lo, hi = CHUNKS[c]
            tag = "rounded%d" % REUSES[c] if c in REUSES else "gathered%d" % c
            gathered = keep.tile([P, PACK, hi - lo], F32, name="gathered%d" % c, tag=tag, align_bytes=64)
            for j in range(PACK):
                step = (hi - lo) // 2 if (c, j) == (0, 0) else hi - lo
                for s0 in range(lo, hi, step):
                    s1 = s0 + step
                    picked = tokens[j][:].indirect(offs_sb[:, s0 // ENTRIES : s1 // ENTRIES])
                    nc.vector.tensor_tensor(gathered[:, j, s0 - lo : s1 - lo], picked, gates[:, s0:s1], MULT)
            x_rounded[c] = keep.tile([P, hi - lo, PACK], BF16, name="rounded%d" % c, tag="rounded%d" % c, align_bytes=64)
            round_and_interleave(x_rounded[c][:], gathered[:])

        def round_w(e0, e1):
            for e in range(e0, e1):
                src = w_raw[:, e, :].rearrange("p (j n) -> p j n", j=PACK)
                round_and_interleave(w_rounded[:, e * N : (e + 1) * N, :], src)

        def quantize(codes, scales, rounded):
            nc.vector.quantize_mx(out=codes.bitcast(FP8X4), scales=scales, in_=rounded.rearrange("p c j -> p (c j)"))

        def quantize_w(pair):
            cols = slice(pair * PAIR * N, (pair + 1) * PAIR * N)
            tag = "tokens2" if pair == WIDE_CHUNKS else "w_codes%d" % pair
            w_codes[pair] = keep.tile([P, PAIR * N], U32, name="w_codes%d" % pair, tag=tag, align_bytes=64)
            quantize(w_codes[pair][:], w_scales[:, cols], w_rounded[:, cols, :])

        def quantize_x(c):
            lo, hi = CHUNKS[c]
            quantize(x_codes[:, lo:hi], x_scales[:, lo:hi], x_rounded[c][:])

        def multiply(c):
            lo, hi = CHUNKS[c]
            for s0 in range(lo, hi, C):
                s1 = min(s0 + C, hi)
                e = s0 // C
                pair, place = divmod(e, PAIR)
                acc = psum.tile([P, s1 - s0], F32, name="acc")
                nc.tensor.matmul_mx(
                    out=acc[:],
                    lhsT=w_codes[pair][:, place * N : (place + 1) * N].bitcast(FP8X4),
                    lhsT_scale=w_scales[:, e * N : (e + 1) * N],
                    rhs=x_codes[:, s0:s1].bitcast(FP8X4),
                    rhs_scale=x_scales[:, s0:s1],
                    start=True,
                    stop=True,
                )
                nc.scalar.activation(y[:, s0:s1], acc[:], RELU, bias=bias[:, e : e + 1])

        nc.sync.dma_start(tokens[0][:], x_rows[:, 0, :])
        nc.sync.dma_start(offs_sb[:], offs)
        load_gate(0, WIDE // 2)
        load_gate(WIDE // 2, WIDE)
        for j in range(1, PACK):
            nc.sync.dma_start(tokens[j][:], x_rows[:, j, :])
        load_gate(WIDE, 2 * WIDE)
        load_w(0, PAIR)
        load_w(PAIR, 2 * PAIR)
        load_gate(2 * WIDE, 4 * WIDE)
        nc.sync.dma_start(bias[:], b)
        load_w(2 * PAIR, 4 * PAIR)
        load_gate(4 * WIDE, S)
        load_w(4 * PAIR, E)
        for r, pos in enumerate((pos1, pos2, pos3)):
            nc.sync.dma_start(pos_sb[r][:], pos)

        gather(0)
        round_w(*W_ROUNDS[0])
        for c in range(1, WIDE_CHUNKS):
            gather(c)
            quantize_x(c - 1)
            quantize_w(c - 1)
            multiply(c - 1)
            if c < len(W_ROUNDS):
                round_w(*W_ROUNDS[c])

        last_wide = WIDE_CHUNKS - 1
        gather(last_wide + 1)
        quantize_w(last_wide)
        gather(last_wide + 2)
        quantize_x(last_wide)
        multiply(last_wide)
        gather(LAST)
        quantize_x(last_wide + 1)
        quantize_w(last_wide + 1)
        multiply(last_wide + 1)
        for c in range(last_wide + 2, LAST + 1):
            quantize_x(c)
            multiply(c)

        pieces = ((0, SPLIT), (SPLIT, T))
        results = [
            [keep.tile([P, hi - lo], F32, name="results%d_%d" % (lo, r)) for r in range(TOP)] for lo, hi in pieces
        ]

        def fetch(piece, r):
            lo, hi = pieces[piece]
            picked = y[:].indirect(pos_sb[r][:, lo // ENTRIES : hi // ENTRIES])
            nc.vector.tensor_copy(results[piece][r][:], picked)

        def add(engine, piece, r, cols):
            total = results[piece][0][:, cols]
            engine.tensor_tensor(total, total, results[piece][r][:, cols], ADD)

        fetch(0, 0)
        for r in range(1, TOP):
            fetch(0, r)
            add(nc.gpsimd, 0, r, slice(0, SPLIT))
        nc.sync.dma_start(out[:, 0:SPLIT], results[0][0][:])

        for r in range(TOP):
            fetch(1, r)
        half = (T - SPLIT) // 2
        for r in range(1, TOP):
            for lo in (0, half):
                add(nc.vector, 1, r, slice(lo, lo + half))
                if r == TOP - 1:
                    nc.sync.dma_start(out[:, SPLIT + lo : SPLIT + lo + half], results[1][0][:, lo : lo + half])
